import numpy as np
import ml_dtypes


def mxq(x, axis, fmt="e4m3"):
    dtype, down = {"e4m3": (ml_dtypes.float8_e4m3fn, 7), "e5m2": (ml_dtypes.float8_e5m2, 14)}[fmt]
    v = np.moveaxis(np.asarray(x, np.float32).astype(ml_dtypes.bfloat16).astype(np.float64), axis, -1)
    blocks = v.reshape(v.shape[:-1] + (-1, 32))
    amax = np.abs(blocks).max(-1, keepdims=True)
    byte = np.maximum(np.where(amax > 0, np.frexp(amax)[1] - 1 + 127, 0) - down, 1)
    scale = np.exp2(byte - 127.0)
    codes = (blocks / scale).astype(np.float32).astype(dtype).astype(np.float64)
    return np.moveaxis((codes * scale).reshape(v.shape), -1, axis)


WIDE = False


def mx_kscale(k):
    if not WIDE:
        return np.ones(k)
    levels = np.array([10, -10, 5, -5, 0])
    if k % 512:
        return np.exp2(np.random.permutation(np.resize(levels, k // 32))).repeat(32)
    a = np.empty((k // 512, 16))
    for p in range(k // 512):
        a[p, :8] = np.random.permutation(np.resize(levels, 8))
        for g in range(8):
            far = levels[np.abs(levels - a[p, g]) >= 10]
            a[p, g + 8] = far[np.random.randint(len(far))]
    return np.exp2(a.ravel()).repeat(32)


def f64(x):
    return np.asarray(x).astype(np.float64)


def striped(idx):
    return np.tile(idx.reshape(-1, 16).T, (8, 1)).astype(np.uint16)


def unstriped(offs):
    return offs[:16].T.reshape(-1).astype(np.int64)


E2M1 = np.array([0.0, 0.5, 1.0, 1.5, 2.0, 3.0, 4.0, 6.0, -0.0, -0.5, -1.0, -1.5, -2.0, -3.0, -4.0, -6.0])


def pack_weight(w, fmt):
    k, n = w.shape
    w = f64(np.asarray(w, np.float32).astype(ml_dtypes.bfloat16)).reshape(k // 32, 32, n)
    amax = np.abs(w).max(1)
    if fmt == "e4m3":
        byte = np.frexp(amax)[1] - 1 + 127 - 7
    else:
        mant, ex = np.frexp(amax / 6.0)
        byte = np.where(mant > 0.5, ex, ex - 1) + 127
    byte = np.clip(np.where(amax > 0, byte, 1), 1, 254)
    scaled = (w * np.exp2(127.0 - byte)[:, None, :]).reshape(k, n).astype(np.float32)
    by_word = np.ascontiguousarray(scaled.reshape(k // 512, 128, 4, n).transpose(0, 1, 3, 2))
    if fmt == "e4m3":
        words = by_word.astype(ml_dtypes.float8_e4m3fn).view(np.uint8)
    else:
        c = by_word.astype(ml_dtypes.float4_e2m1fn).view(np.uint8) & 0xF
        words = (c[..., 0::2] | (c[..., 1::2] << 4)).reshape(k // 512, 128, 2 * n)
    return np.ascontiguousarray(words), np.ascontiguousarray(byte.astype(np.uint8).reshape(k // 512, 16, n))


def unpack_weight(words, scales, fmt):
    g, _, n = scales.shape
    words = np.ascontiguousarray(words).reshape(g, 128, n, -1)
    if fmt == "e4m3":
        vals = words.view(ml_dtypes.float8_e4m3fn).astype(np.float64)
    else:
        nib = np.empty((g, 128, n, 4), np.uint8)
        nib[..., 0::2] = words & 0xF
        nib[..., 1::2] = words >> 4
        vals = E2M1[nib]
    vals = vals * np.repeat(np.exp2(scales.astype(np.float64) - 127.0), 8, axis=1)[..., None]
    return vals.transpose(0, 1, 3, 2).reshape(g * 512, n)


def gelu(v):
    return 0.5 * v * (1.0 + np.tanh(np.sqrt(2.0 / np.pi) * (v + 0.044715 * v**3)))


def striped8(idx):
    return np.concatenate([v.reshape(-1, 16).T for v in idx]).astype(np.uint16)


def unstriped8(offs):
    return np.stack([offs[16 * g:16 * g + 16].T.reshape(-1) for g in range(8)]).astype(np.int64)


def heads(xT, wgt, idx8):
    k = np.arange(xT.shape[0])
    return wgt[k // 4 % 128] * xT[k[:, None], idx8[k % 512 // 64]]


K, T, S, H, N, G, P = 1024, 2048, 1024, 1024, 512, 8, 128

def setup_inputs():
    n = np.random.standard_normal
    s = mx_kscale(K)[:, None]
    u = mx_kscale(H)[:, None]
    xT = (n((K, T)) * s).astype(np.float32)
    wgt = np.repeat(np.random.uniform(0.5, 2.0, (G, S)), P // G, axis=0).astype(np.float32)
    offs = striped8(np.stack([np.random.permutation(T)[:S] for _ in range(G)]))
    wgate_words, wgate_scales = pack_weight(n((K, H)) / np.sqrt(K) / s, "e2m1")
    bgate = (0.5 * n(H)).astype(np.float32)
    wval = (n((K, H)) / np.sqrt(K) / s * u.T).astype(np.float32)
    wproj_words, wproj_scales = pack_weight(n((H, N)) / np.sqrt(H) / u, "e4m3")
    bproj = (0.5 * n(N)).astype(np.float32)
    return {"xT": xT, "wgt": wgt, "offs": offs,
            "wgate_words": wgate_words, "wgate_scales": wgate_scales, "bgate": bgate,
            "wval": wval, "wproj_words": wproj_words, "wproj_scales": wproj_scales,
            "bproj": bproj}

def reference(xT, wgt, offs, wgate_words, wgate_scales, bgate, wval, wproj_words, wproj_scales, bproj):
    xg = heads(f64(xT), f64(wgt), unstriped8(offs))
    xq = mxq(xg, 0, "e4m3")
    wgate = unpack_weight(wgate_words, wgate_scales, "e2m1")
    wproj = unpack_weight(wproj_words, wproj_scales, "e4m3")
    a = (wgate.T @ xq) + f64(bgate)[:, None]
    val = mxq(f64(wval), 0, "e4m3").T @ xq
    h = val * (1.0 / (1.0 + np.exp(-a)))
    return (wproj.T @ mxq(h, 0, "e4m3")) + f64(bproj)[:, None]

@@ -1,0 +1,285 @@
+from contextlib import ExitStack
+
+import concourse.mybir as mybir
+
+K, T, S, H, N = 1024, 2048, 1024, 1024, 512
+FLOPS = 2 * K * H * S * 2 + 2 * H * N * S
+
+F32 = mybir.dt.float32
+BF16 = mybir.dt.bfloat16
+I32 = mybir.dt.int32
+U32 = mybir.dt.uint32
+U16 = mybir.dt.uint16
+U8 = mybir.dt.uint8
+FP8X4 = mybir.dt.float8_e4m3fn_x4
+FP4X4 = mybir.dt.float4_e2m1fn_x4
+MULT = mybir.AluOpType.mult
+ADD = mybir.AluOpType.add
+SIGMOID = mybir.ActivationFunctionType.Sigmoid
+IDENTITY = mybir.ActivationFunctionType.Identity
+
+P = 128
+PACK = 4
+KP = P * PACK
+HALF = 512
+QUARTER = 256
+CHUNK = 128
+BANKS = 8
+
+
+def tile_list_head_picked_glu_kernel(
+    tc, xT, wgt, offs, wgate_words, wgate_scales, bgate, wval, wproj_words, wproj_scales, bproj, out
+):
+    nc = tc.nc
+    with ExitStack() as ctx:
+        keep = ctx.enter_context(tc.tile_pool(name="keep", bufs=1))
+        psum = ctx.enter_context(tc.psum_pool(name="psum", bufs=1))
+        banks_taken = []
+
+        def next_bank(shape):
+            i = len(banks_taken) % BANKS
+            banks_taken.append(i)
+            return psum.tile(shape, F32, name="bank%d" % i)
+
+        def sb(shape, dtype, name, tag=None):
+            return keep.tile(shape, dtype, name=name, tag=tag or name, align_bytes=64)
+
+        def load_scale_rows(plane, scales):
+            rows = scales.bitcast(I32)
+            words = plane[:].bitcast(I32).rearrange("p (a c) -> p a c", a=2)
+            for q in range(4):
+                nc.sync.dma_start(
+                    out=words[32 * q : 32 * q + 4], in_=rows[:, 4 * q : 4 * q + 4, :].rearrange("a r c -> r a c")
+                )
+
+        def weave(engine_copy, dst, src):
+            engine_copy(
+                out=dst.rearrange("p (c i) t -> p c t i", i=4), in_=src.rearrange("p t (c i) -> p c t i", i=4)
+            )
+
+        def quantize(name, grouped, width):
+            codes = sb([P, width], U32, name + "_codes")
+            scales = sb([P, width], U8, name + "_scales")
+            nc.vector.quantize_mx(out=codes[:].bitcast(FP8X4), scales=scales[:], in_=grouped)
+            return codes, scales
+
+        warm_in = sb([P, 1], F32, "warm_in")
+        warm_out = sb([P, 1], F32, "warm_out")
+        nc.gpsimd.memset(warm_in[:], 0.0)
+        nc.scalar.activation(warm_out[:], warm_in[:], SIGMOID)
+
+        gs_raw = sb([P, 2 * H], U8, "gs_raw")
+        nc.vector.memset(gs_raw[:].bitcast(I32), 0)
+        ps_plane = sb([P, 2 * N], U8, "ps_plane")
+        nc.gpsimd.memset(ps_plane[:].bitcast(I32), 0)
+
+        offsets = keep.tile([P, S // 16], U16, name="offsets")
+        nc.sync.dma_start(offsets[:], offs)
+        gw_raw = sb([P, 2 * 2 * H], U8, "gw_raw")
+        nc.sync.dma_start(
+            out=gw_raw[:].bitcast(I32).rearrange("p (a c) -> p a c", a=2),
+            in_=wgate_words.bitcast(I32).rearrange("a p c -> p a c"),
+        )
+        load_scale_rows(gs_raw, wgate_scales)
+        wgt_sb = sb([P, S], F32, "wgt_sb")
+        nc.sync.dma_start(out=wgt_sb[:, :HALF], in_=wgt[:, :HALF])
+
+        wv_raw = {}
+
+        def load_wval(a, b):
+            raw = sb([P, PACK, HALF], F32, "wv_raw%d%d" % (a, b), tag="big%d" % (2 * b + a))
+            nc.sync.dma_start(
+                out=raw[:],
+                in_=wval[a * KP : (a + 1) * KP, b * HALF : (b + 1) * HALF].rearrange("(p j) c -> p j c", j=PACK),
+            )
+            wv_raw[a, b] = raw
+
+        wq = {}
+
+        def quantize_wval(copy, a, b):
+            wb = sb([P, PACK, P, PACK], BF16, "wv_bf%d%d" % (a, b))
+            copy(
+                out=wb[:].rearrange("p t m j -> p m j t"),
+                in_=wv_raw[a, b][:].rearrange("p j (m t) -> p m j t", t=PACK),
+            )
+            wq[a, b] = quantize("wq%d%d" % (a, b), wb[:].rearrange("p t m j -> p (t m j)"), HALF)
+
+        x_rows = xT.rearrange("(a p i) t -> a i p t", a=2, i=PACK)
+        planes = []
+
+        def load_plane(n):
+            plane = sb([P, T], F32, "x%d" % n, tag="big%d" % n)
+            nc.sync.dma_start(out=plane[:], in_=x_rows[n // 4, n % 4])
+            planes.append(plane)
+
+        load_plane(0)
+        nc.sync.dma_start(out=wgt_sb[:, HALF:], in_=wgt[:, HALF:])
+        for n in range(1, 6):
+            load_plane(n)
+        wv00 = sb([P, PACK, HALF], F32, "wv00")
+        nc.sync.dma_start(out=wv00[:], in_=wval[:KP, :HALF].rearrange("(p j) c -> p j c", j=PACK))
+        wv_raw[0, 0] = wv00
+        for n in range(6, 8):
+            load_plane(n)
+        bg = sb([P, 2, PACK], F32, "bg")
+        nc.sync.dma_start(out=bg[:], in_=bgate.rearrange("(b p t) -> p b t", b=2, t=PACK))
+
+        gw = sb([P, 2 * 2 * H], U8, "gw")
+        nc.vector.tensor_copy(
+            out=gw[:].bitcast(U16).rearrange("p (g t u v) -> p g u t v", g=4, t=4, v=8),
+            in_=gw_raw[:].bitcast(U16).rearrange("p (g u v t) -> p g u t v", g=4, t=4, v=8),
+        )
+        gs = sb([P, 2 * H], U8, "gs")
+        nc.vector.tensor_copy(
+            out=gs[:].rearrange("p (g t u v) -> p g u t v", g=4, t=4, v=16),
+            in_=gs_raw[:].rearrange("p (g u v t) -> p g u t v", g=4, t=4, v=16),
+        )
+
+        def gather(dst, n, lo, hi):
+            nc.vector.tensor_tensor(
+                dst[:, n % 4, lo:hi], planes[n][:].indirect(offsets[:, lo // 16 : hi // 16]), wgt_sb[:, lo:hi], MULT
+            )
+
+        xq = {}
+        picked0 = sb([P, PACK, S], F32, "picked0")
+        gather(picked0, 0, 0, HALF)
+        gather(picked0, 0, HALF, S)
+        for n in range(1, 4):
+            gather(picked0, n, 0, S)
+        shared = sb([P, PACK * S + HALF], F32, "shared")
+        picked1 = shared[:, : PACK * S].rearrange("p (t j) -> p t j", t=PACK)
+        for hf in range(2):
+            xb = sb([P, HALF, PACK], BF16, "xb0_%d" % hf)
+            weave(nc.scalar.copy, xb[:], picked0[:, :, hf * HALF : (hf + 1) * HALF])
+            gather(picked1, 4 + hf, 0, S)
+            xq[0, hf] = quantize("xq0_%d" % hf, xb[:].rearrange("p j t -> p (j t)"), HALF)
+        gather(picked1, 6, 0, S)
+        quantize_wval(nc.scalar.copy, 0, 0)
+        gather(picked1, 7, 0, HALF)
+
+        def gate_pass(bank, a, b, t, hf):
+            col = (a * 2 + b) * HALF + t * P
+            codes, scales = xq[a, hf]
+            nc.tensor.matmul_mx(
+                out=bank[:],
+                lhsT=gw[:, 2 * col : 2 * (col + P)].bitcast(FP4X4),
+                lhsT_scale=gs[:, col : col + P],
+                rhs=codes[:].bitcast(FP8X4),
+                rhs_scale=scales[:],
+                start=(a == 0),
+                stop=(a == 1),
+            )
+
+        gate_banks = [next_bank([P, HALF]) for u in range(8)]
+        for u in range(8):
+            gate_pass(gate_banks[u], 0, u // 4, u % 4, 0)
+
+        xb_flat = shared[:, PACK * S - HALF :].bitcast(BF16)
+        xb = xb_flat.rearrange("p (j t) -> p j t", t=PACK)
+        weave(nc.scalar.copy, xb[:, :QUARTER], picked1[:, :, :QUARTER])
+        weave(nc.vector.tensor_copy, xb[:, QUARTER:], picked1[:, :, QUARTER:HALF])
+        xq[1, 0] = quantize("xq1_0", xb_flat, HALF)
+        gather(picked1, 7, HALF, S)
+        xb = sb([P, HALF, PACK], BF16, "xb1_1")
+        weave(nc.vector.tensor_copy, xb[:], picked1[:, :, HALF:])
+        xq[1, 1] = quantize("xq1_1", xb[:].rearrange("p j t -> p (j t)"), HALF)
+
+        load_wval(1, 0)
+        load_wval(0, 1)
+        load_wval(1, 1)
+        quantize_wval(nc.vector.tensor_copy, 1, 0)
+        quantize_wval(nc.vector.tensor_copy, 0, 1)
+        quantize_wval(nc.vector.tensor_copy, 1, 1)
+
+        pw = sb([P, 2 * N], U32, "pw")
+        nc.sync.dma_start(
+            out=pw[:].bitcast(I32).rearrange("p (a c) -> p a c", a=2),
+            in_=wproj_words.rearrange("a p c i -> p a (c i)").bitcast(I32),
+        )
+        load_scale_rows(ps_plane, wproj_scales)
+        bp = sb([P, N // P], F32, "bp")
+        with nc.allow_non_contiguous_dma(reason="one bias value a partition"):
+            nc.sync.dma_start(out=bp[:], in_=bproj.rearrange("(i p) -> p i", p=P))
+
+        sig = {}
+
+        def sigmoid(bank, b, t, hf):
+            if t == 0:
+                sig[b, hf] = sb([P, PACK, HALF], F32, "sig%d%d" % (b, hf), tag="big%d" % (4 + 2 * hf + b))
+            nc.scalar.activation(sig[b, hf][:, t, :], bank[:], SIGMOID, bias=bg[:, b, t : t + 1])
+
+        for u in range(8):
+            gate_pass(gate_banks[u], 1, u // 4, u % 4, 0)
+            sigmoid(gate_banks[u], u // 4, u % 4, 0)
+
+        gate_banks = [next_bank([P, HALF]) for u in range(8)]
+        for u in range(8):
+            gate_pass(gate_banks[u], 0, u // 4, u % 4, 1)
+        for u in range(8):
+            gate_pass(gate_banks[u], 1, u // 4, u % 4, 1)
+            sigmoid(gate_banks[u], u // 4, u % 4, 1)
+
+        def hidden(b, lo, width):
+            hf, base = divmod(lo, HALF)
+            hb = sb([P, width, PACK], BF16, "hb%d_%d" % (b, lo))
+            for c in range(0, width, CHUNK):
+                bank = next_bank([P, PACK, CHUNK])
+                cols = slice(base + c, base + c + CHUNK)
+                for t in range(PACK):
+                    for a in range(2):
+                        w_codes, w_scales = wq[a, b]
+                        codes, scales = xq[a, hf]
+                        nc.tensor.matmul_mx(
+                            out=bank[:, t, :],
+                            lhsT=w_codes[:, t * P : (t + 1) * P].bitcast(FP8X4),
+                            lhsT_scale=w_scales[:, t * P : (t + 1) * P],
+                            rhs=codes[:, cols].bitcast(FP8X4),
+                            rhs_scale=scales[:, cols],
+                            start=(a == 0),
+                            stop=(a == 1),
+                        )
+                nc.vector.tensor_tensor(
+                    hb[:, c : c + CHUNK, :].rearrange("p (c i) t -> p c t i", i=4),
+                    bank[:].rearrange("p t (c i) -> p c t i", i=4),
+                    sig[b, hf][:, :, cols].rearrange("p t (c i) -> p c t i", i=4),
+                    MULT,
+                )
+            return quantize("hq%d_%d" % (b, lo), hb[:].rearrange("p j t -> p (j t)"), width)
+
+        out_rows = out.rearrange("(i p) j -> p i j", p=P)
+
+        def project(hq, lo, width, last):
+            per_bank = min(HALF // width, 2)
+            for i0 in range(0, N // P, per_bank):
+                bank = next_bank([P, per_bank, width])
+                res = sb([P, per_bank, width], F32, "res%d_%d" % (lo, i0))
+                for i in range(i0, i0 + per_bank):
+                    for b in range(2):
+                        codes, scales, c0 = hq[b]
+                        col = b * N + i * P
+                        nc.tensor.matmul_mx(
+                            out=bank[:, i - i0, :],
+                            lhsT=pw[:, col : col + P].bitcast(FP8X4),
+                            lhsT_scale=ps_plane[:, col : col + P],
+                            rhs=codes[:, c0 : c0 + width].bitcast(FP8X4),
+                            rhs_scale=scales[:, c0 : c0 + width],
+                            start=(b == 0),
+                            stop=(b == 1),
+                        )
+                for i in range(i0, i0 + per_bank):
+                    if last and i0 > 0:
+                        nc.vector.tensor_scalar(res[:, i - i0, :], bank[:, i - i0, :], bp[:, i : i + 1], None, ADD)
+                    else:
+                        nc.scalar.activation(res[:, i - i0, :], bank[:, i - i0, :], IDENTITY, bias=bp[:, i : i + 1])
+                nc.sync.dma_start(out=out_rows[:, i0 : i0 + per_bank, lo : lo + width], in_=res[:])
+
+        h00 = hidden(0, 0, HALF)
+        h10 = hidden(1, 0, HALF)
+        h01 = hidden(0, HALF, HALF)
+        h12 = hidden(1, HALF, QUARTER)
+        project([h00 + (0,), h10 + (0,)], 0, HALF, False)
+        h13 = hidden(1, HALF + QUARTER, CHUNK)
+        h14 = hidden(1, HALF + QUARTER + CHUNK, CHUNK)
+        project([h01 + (0,), h12 + (0,)], HALF, QUARTER, False)
+        project([h01 + (QUARTER,), h13 + (0,)], HALF + QUARTER, CHUNK, False)
+        project([h01 + (QUARTER + CHUNK,), h14 + (0,)], HALF + QUARTER + CHUNK, CHUNK, True)

@@ -57,8 +57,8 @@ def tile_list_head_picked_glu_kernel(
                 out=dst.rearrange("p (c i) t -> p c t i", i=4), in_=src.rearrange("p t (c i) -> p c t i", i=4)
             )
 
-        def quantize(name, grouped, width):
-            codes = sb([P, width], U32, name + "_codes")
+        def quantize(name, grouped, width, tag=None):
+            codes = sb([P, width], U32, name + "_codes", tag=tag)
             scales = sb([P, width], U8, name + "_scales")
             nc.vector.quantize_mx(out=codes[:].bitcast(FP8X4), scales=scales[:], in_=grouped)
             return codes, scales
@@ -82,7 +82,7 @@ def tile_list_head_picked_glu_kernel(
         )
         load_scale_rows(gs_raw, wgate_scales)
         wgt_sb = sb([P, S], F32, "wgt_sb")
-        nc.sync.dma_start(out=wgt_sb[:, :HALF], in_=wgt[:, :HALF])
+        nc.sync.dma_start(out=wgt_sb[:, :QUARTER], in_=wgt[:, :QUARTER])
 
         wv_raw = {}
 
@@ -96,13 +96,18 @@ def tile_list_head_picked_glu_kernel(
 
         wq = {}
 
-        def quantize_wval(copy, a, b):
+        wv_bf = {}
+
+        def round_wval(copy, a, b):
             wb = sb([P, PACK, P, PACK], BF16, "wv_bf%d%d" % (a, b))
             copy(
                 out=wb[:].rearrange("p t m j -> p m j t"),
                 in_=wv_raw[a, b][:].rearrange("p j (m t) -> p m j t", t=PACK),
             )
-            wq[a, b] = quantize("wq%d%d" % (a, b), wb[:].rearrange("p t m j -> p (t m j)"), HALF)
+            wv_bf[a, b] = wb[:].rearrange("p t m j -> p (t m j)")
+
+        def quantize_wval(a, b, tag=None):
+            wq[a, b] = quantize("wq%d%d" % (a, b), wv_bf[a, b], HALF, tag=tag)
 
         x_rows = xT.rearrange("(a p i) t -> a i p t", a=2, i=PACK)
         planes = []
@@ -113,14 +118,13 @@ def tile_list_head_picked_glu_kernel(
             planes.append(plane)
 
         load_plane(0)
-        nc.sync.dma_start(out=wgt_sb[:, HALF:], in_=wgt[:, HALF:])
-        for n in range(1, 6):
+        nc.sync.dma_start(out=wgt_sb[:, QUARTER:], in_=wgt[:, QUARTER:])
+        for n in range(1, 7):
             load_plane(n)
         wv00 = sb([P, PACK, HALF], F32, "wv00")
         nc.sync.dma_start(out=wv00[:], in_=wval[:KP, :HALF].rearrange("(p j) c -> p j c", j=PACK))
         wv_raw[0, 0] = wv00
-        for n in range(6, 8):
-            load_plane(n)
+        load_plane(7)
         bg = sb([P, 2, PACK], F32, "bg")
         nc.sync.dma_start(out=bg[:], in_=bgate.rearrange("(b p t) -> p b t", b=2, t=PACK))
 
@@ -142,19 +146,22 @@ def tile_list_head_picked_glu_kernel(
 
         xq = {}
         picked0 = sb([P, PACK, S], F32, "picked0")
-        gather(picked0, 0, 0, HALF)
+        gather(picked0, 0, 0, QUARTER)
+        gather(picked0, 0, QUARTER, HALF)
         gather(picked0, 0, HALF, S)
         for n in range(1, 4):
             gather(picked0, n, 0, S)
-        shared = sb([P, PACK * S + HALF], F32, "shared")
-        picked1 = shared[:, : PACK * S].rearrange("p (t j) -> p t j", t=PACK)
+        shared = sb([P, PACK * S], F32, "shared")
+        picked1 = shared[:].rearrange("p (t j) -> p t j", t=PACK)
+        xb0 = []
         for hf in range(2):
             xb = sb([P, HALF, PACK], BF16, "xb0_%d" % hf)
             weave(nc.scalar.copy, xb[:], picked0[:, :, hf * HALF : (hf + 1) * HALF])
             gather(picked1, 4 + hf, 0, S)
-            xq[0, hf] = quantize("xq0_%d" % hf, xb[:].rearrange("p j t -> p (j t)"), HALF)
+            xb0.append(xb[:].rearrange("p j t -> p (j t)"))
+        xq[0, 0] = quantize("xq0_0", xb0[0], HALF)
         gather(picked1, 6, 0, S)
-        quantize_wval(nc.scalar.copy, 0, 0)
+        round_wval(nc.scalar.copy, 0, 0)
         gather(picked1, 7, 0, HALF)
 
         def gate_pass(bank, a, b, t, hf):
@@ -174,22 +181,32 @@ def tile_list_head_picked_glu_kernel(
         for u in range(8):
             gate_pass(gate_banks[u], 0, u // 4, u % 4, 0)
 
-        xb_flat = shared[:, PACK * S - HALF :].bitcast(BF16)
-        xb = xb_flat.rearrange("p (j t) -> p j t", t=PACK)
-        weave(nc.scalar.copy, xb[:, :QUARTER], picked1[:, :, :QUARTER])
-        weave(nc.vector.tensor_copy, xb[:, QUARTER:], picked1[:, :, QUARTER:HALF])
-        xq[1, 0] = quantize("xq1_0", xb_flat, HALF)
+        codes = sb([P, HALF], U32, "xq1_0_codes")
+        scales = sb([P, HALF], U8, "xq1_0_scales")
+        xq[1, 0] = codes, scales
+        by_scalar = shared[:, PACK * S - HALF :].bitcast(BF16)
+        by_vector = sb([P, QUARTER * PACK], BF16, "by_vector")
+        weave(nc.scalar.copy, by_scalar.rearrange("p (j t) -> p j t", t=PACK), picked1[:, :, :QUARTER])
+        weave(nc.vector.tensor_copy, by_vector[:].rearrange("p (j t) -> p j t", t=PACK), picked1[:, :, QUARTER:HALF])
+        nc.vector.quantize_mx(out=codes[:, QUARTER:].bitcast(FP8X4), scales=scales[:, QUARTER:], in_=by_vector[:])
+        nc.vector.quantize_mx(out=codes[:, :QUARTER].bitcast(FP8X4), scales=scales[:, :QUARTER], in_=by_scalar)
         gather(picked1, 7, HALF, S)
+        xq[0, 1] = quantize("xq0_1", xb0[1], HALF, tag="big7")
         xb = sb([P, HALF, PACK], BF16, "xb1_1")
-        weave(nc.vector.tensor_copy, xb[:], picked1[:, :, HALF:])
+        weave(nc.scalar.copy, xb[:, :QUARTER], picked1[:, :, HALF : HALF + QUARTER])
+        weave(nc.vector.tensor_copy, xb[:, QUARTER:], picked1[:, :, HALF + QUARTER :])
         xq[1, 1] = quantize("xq1_1", xb[:].rearrange("p j t -> p (j t)"), HALF)
 
         load_wval(1, 0)
         load_wval(0, 1)
         load_wval(1, 1)
-        quantize_wval(nc.vector.tensor_copy, 1, 0)
-        quantize_wval(nc.vector.tensor_copy, 0, 1)
-        quantize_wval(nc.vector.tensor_copy, 1, 1)
+        round_wval(nc.vector.tensor_copy, 1, 0)
+        quantize_wval(0, 0, tag="xb0_1")
+        round_wval(nc.vector.tensor_copy, 0, 1)
+        quantize_wval(1, 0)
+        round_wval(nc.vector.tensor_copy, 1, 1)
+        quantize_wval(0, 1)
+        quantize_wval(1, 1)
 
         pw = sb([P, 2 * N], U32, "pw")
         nc.sync.dma_start(
@@ -205,7 +222,7 @@ def tile_list_head_picked_glu_kernel(
 
         def sigmoid(bank, b, t, hf):
             if t == 0:
-                sig[b, hf] = sb([P, PACK, HALF], F32, "sig%d%d" % (b, hf), tag="big%d" % (4 + 2 * hf + b))
+                sig[b, hf] = sb([P, PACK, HALF], F32, "sig%d%d" % (b, hf), tag="big%d" % ((4 + 2 * hf + b) % 7))
             nc.scalar.activation(sig[b, hf][:, t, :], bank[:], SIGMOID, bias=bg[:, b, t : t + 1])
 
         for u in range(8):
@@ -239,9 +256,9 @@ def tile_list_head_picked_glu_kernel(
                             stop=(a == 1),
                         )
                 nc.vector.tensor_tensor(
-                    hb[:, c : c + CHUNK, :].rearrange("p (c i) t -> p c t i", i=4),
-                    bank[:].rearrange("p t (c i) -> p c t i", i=4),
-                    sig[b, hf][:, :, cols].rearrange("p t (c i) -> p c t i", i=4),
+                    hb[:, c : c + CHUNK, :].rearrange("p (c i) t -> p c t i", i=2),
+                    bank[:].rearrange("p t (c i) -> p c t i", i=2),
+                    sig[b, hf][:, :, cols].rearrange("p t (c i) -> p c t i", i=2),
                     MULT,
                 )
             return quantize("hq%d_%d" % (b, lo), hb[:].rearrange("p j t -> p (j t)"), width)

@@ -121,10 +121,26 @@ def tile_list_head_picked_glu_kernel(
         nc.sync.dma_start(out=wgt_sb[:, QUARTER:], in_=wgt[:, QUARTER:])
         for n in range(1, 7):
             load_plane(n)
-        wv00 = sb([P, PACK, HALF], F32, "wv00")
-        nc.sync.dma_start(out=wv00[:], in_=wval[:KP, :HALF].rearrange("(p j) c -> p j c", j=PACK))
-        wv_raw[0, 0] = wv00
+        wv00 = []
+
+        def load_wv00(part):
+            raw = sb([P, PACK, QUARTER], F32, "wv00_%d" % part)
+            cols = slice(part * QUARTER, (part + 1) * QUARTER)
+            nc.sync.dma_start(out=raw[:], in_=wval[:KP, cols].rearrange("(p j) c -> p j c", j=PACK))
+            wv00.append(raw)
+
+        wb00 = sb([P, PACK, P, PACK], BF16, "wv_bf00")
+        wv_bf[0, 0] = wb00[:].rearrange("p t m j -> p (t m j)")
+
+        def round_wv00(copy, part):
+            copy(
+                out=wb00[:, :, part * 64 : (part + 1) * 64, :].rearrange("p t m j -> p m j t"),
+                in_=wv00[part][:].rearrange("p j (m t) -> p m j t", t=PACK),
+            )
+
+        load_wv00(0)
         load_plane(7)
+        load_wv00(1)
         bg = sb([P, 2, PACK], F32, "bg")
         nc.sync.dma_start(out=bg[:], in_=bgate.rearrange("(b p t) -> p b t", b=2, t=PACK))
 
@@ -159,10 +175,11 @@ def tile_list_head_picked_glu_kernel(
             weave(nc.scalar.copy, xb[:], picked0[:, :, hf * HALF : (hf + 1) * HALF])
             gather(picked1, 4 + hf, 0, S)
             xb0.append(xb[:].rearrange("p j t -> p (j t)"))
-        xq[0, 0] = quantize("xq0_0", xb0[0], HALF)
         gather(picked1, 6, 0, S)
-        round_wval(nc.scalar.copy, 0, 0)
-        gather(picked1, 7, 0, HALF)
+        xq[0, 0] = quantize("xq0_0", xb0[0], HALF, tag="big6")
+        round_wv00(nc.scalar.copy, 0)
+        gather(picked1, 7, 0, QUARTER)
+        gather(picked1, 7, QUARTER, HALF)
 
         def gate_pass(bank, a, b, t, hf):
             col = (a * 2 + b) * HALF + t * P
@@ -188,8 +205,9 @@ def tile_list_head_picked_glu_kernel(
         by_vector = sb([P, QUARTER * PACK], BF16, "by_vector")
         weave(nc.scalar.copy, by_scalar.rearrange("p (j t) -> p j t", t=PACK), picked1[:, :, :QUARTER])
         weave(nc.vector.tensor_copy, by_vector[:].rearrange("p (j t) -> p j t", t=PACK), picked1[:, :, QUARTER:HALF])
-        nc.vector.quantize_mx(out=codes[:, QUARTER:].bitcast(FP8X4), scales=scales[:, QUARTER:], in_=by_vector[:])
         nc.vector.quantize_mx(out=codes[:, :QUARTER].bitcast(FP8X4), scales=scales[:, :QUARTER], in_=by_scalar)
+        nc.vector.quantize_mx(out=codes[:, QUARTER:].bitcast(FP8X4), scales=scales[:, QUARTER:], in_=by_vector[:])
+        round_wv00(nc.scalar.copy, 1)
         gather(picked1, 7, HALF, S)
         xq[0, 1] = quantize("xq0_1", xb0[1], HALF, tag="big7")
         xb = sb([P, HALF, PACK], BF16, "xb1_1")
@@ -222,7 +240,7 @@ def tile_list_head_picked_glu_kernel(
 
         def sigmoid(bank, b, t, hf):
             if t == 0:
-                sig[b, hf] = sb([P, PACK, HALF], F32, "sig%d%d" % (b, hf), tag="big%d" % ((4 + 2 * hf + b) % 7))
+                sig[b, hf] = sb([P, PACK, HALF], F32, "sig%d%d" % (b, hf), tag=("big4", "big5", "big0", None)[2 * hf + b])
             nc.scalar.activation(sig[b, hf][:, t, :], bank[:], SIGMOID, bias=bg[:, b, t : t + 1])
 
         for u in range(8):

@@ -20,11 +20,16 @@ IDENTITY = mybir.ActivationFunctionType.Identity
 
 P = 128
 PACK = 4
-KP = P * PACK
-HALF = 512
-QUARTER = 256
-CHUNK = 128
+PASS = P * PACK
+PASSES = 2
+PLANES = PASSES * PACK
+HALF = S // 2
+QUARTER = S // 4
+CHUNK = HALF // PACK
+LIST_ROWS = 16
 BANKS = 8
+OUT_TILES = N // P
+LINE = 16
 
 
 def tile_list_head_picked_glu_kernel(
@@ -37,284 +42,274 @@ def tile_list_head_picked_glu_kernel(
         banks_taken = []
 
         def next_bank(shape):
-            i = len(banks_taken) % BANKS
-            banks_taken.append(i)
-            return psum.tile(shape, F32, name="bank%d" % i)
+            index = len(banks_taken) % BANKS
+            banks_taken.append(index)
+            return psum.tile(shape, F32, name="bank%d" % index)
 
-        def sb(shape, dtype, name, tag=None):
+        def sbuf(shape, dtype, name, tag=None):
             return keep.tile(shape, dtype, name=name, tag=tag or name, align_bytes=64)
 
-        def load_scale_rows(plane, scales):
-            rows = scales.bitcast(I32)
-            words = plane[:].bitcast(I32).rearrange("p (a c) -> p a c", a=2)
-            for q in range(4):
+        def load_scale_rows(scale_tile, scale_rows):
+            src = scale_rows.bitcast(I32)
+            dst = scale_tile[:].bitcast(I32).rearrange("p (a c) -> p a c", a=PASSES)
+            for quad in range(4):
                 nc.sync.dma_start(
-                    out=words[32 * q : 32 * q + 4], in_=rows[:, 4 * q : 4 * q + 4, :].rearrange("a r c -> r a c")
+                    out=dst[32 * quad : 32 * quad + 4],
+                    in_=src[:, 4 * quad : 4 * quad + 4, :].rearrange("a s c -> s a c"),
                 )
 
-        def weave(engine_copy, dst, src):
-            engine_copy(
-                out=dst.rearrange("p (c i) t -> p c t i", i=4), in_=src.rearrange("p t (c i) -> p c t i", i=4)
-            )
+        def weave(copy, dst, src):
+            copy(out=dst.rearrange("p (c e) i -> p c i e", e=4), in_=src.rearrange("p i (c e) -> p c i e", e=4))
 
-        def quantize(name, grouped, width, tag=None):
-            codes = sb([P, width], U32, name + "_codes", tag=tag)
-            scales = sb([P, width], U8, name + "_scales")
-            nc.vector.quantize_mx(out=codes[:].bitcast(FP8X4), scales=scales[:], in_=grouped)
+        def quantize(name, woven, width, tag=None):
+            codes = sbuf([P, width], U32, name + "_codes", tag=tag)
+            scales = sbuf([P, width], U8, name + "_scales")
+            nc.vector.quantize_mx(out=codes[:].bitcast(FP8X4), scales=scales[:], in_=woven)
             return codes, scales
 
-        warm_in = sb([P, 1], F32, "warm_in")
-        warm_out = sb([P, 1], F32, "warm_out")
-        nc.gpsimd.memset(warm_in[:], 0.0)
-        nc.scalar.activation(warm_out[:], warm_in[:], SIGMOID)
+        gate_scales_raw = sbuf([P, PASSES * H], U8, "gate_scales_raw")
+        nc.vector.memset(gate_scales_raw[:].bitcast(I32), 0)
+        proj_scales = sbuf([P, PASSES * N], U8, "proj_scales")
+        nc.gpsimd.memset(proj_scales[:].bitcast(I32), 0)
 
-        gs_raw = sb([P, 2 * H], U8, "gs_raw")
-        nc.vector.memset(gs_raw[:].bitcast(I32), 0)
-        ps_plane = sb([P, 2 * N], U8, "ps_plane")
-        nc.gpsimd.memset(ps_plane[:].bitcast(I32), 0)
-
-        offsets = keep.tile([P, S // 16], U16, name="offsets")
+        offsets = keep.tile([P, S // LIST_ROWS], U16, name="offsets")
         nc.sync.dma_start(offsets[:], offs)
-        gw_raw = sb([P, 2 * 2 * H], U8, "gw_raw")
+        gate_words_raw = sbuf([P, PASSES * 2 * H], U8, "gate_words_raw")
         nc.sync.dma_start(
-            out=gw_raw[:].bitcast(I32).rearrange("p (a c) -> p a c", a=2),
+            out=gate_words_raw[:].bitcast(I32).rearrange("p (a c) -> p a c", a=PASSES),
             in_=wgate_words.bitcast(I32).rearrange("a p c -> p a c"),
         )
-        load_scale_rows(gs_raw, wgate_scales)
-        wgt_sb = sb([P, S], F32, "wgt_sb")
-        nc.sync.dma_start(out=wgt_sb[:, :QUARTER], in_=wgt[:, :QUARTER])
+        load_scale_rows(gate_scales_raw, wgate_scales)
+        weights = sbuf([P, S], F32, "weights")
+        nc.sync.dma_start(out=weights[:, :QUARTER], in_=wgt[:, :QUARTER])
 
-        wv_raw = {}
-
-        def load_wval(a, b):
-            raw = sb([P, PACK, HALF], F32, "wv_raw%d%d" % (a, b), tag="big%d" % (2 * b + a))
-            nc.sync.dma_start(
-                out=raw[:],
-                in_=wval[a * KP : (a + 1) * KP, b * HALF : (b + 1) * HALF].rearrange("(p j) c -> p j c", j=PACK),
-            )
-            wv_raw[a, b] = raw
-
-        wq = {}
-
-        wv_bf = {}
-
-        def round_wval(copy, a, b):
-            wb = sb([P, PACK, P, PACK], BF16, "wv_bf%d%d" % (a, b))
-            copy(
-                out=wb[:].rearrange("p t m j -> p m j t"),
-                in_=wv_raw[a, b][:].rearrange("p j (m t) -> p m j t", t=PACK),
-            )
-            wv_bf[a, b] = wb[:].rearrange("p t m j -> p (t m j)")
-
-        def quantize_wval(a, b, tag=None):
-            wq[a, b] = quantize("wq%d%d" % (a, b), wv_bf[a, b], HALF, tag=tag)
-
-        x_rows = xT.rearrange("(a p i) t -> a i p t", a=2, i=PACK)
+        x_rows = xT.rearrange("(a p i) t -> a i p t", a=PASSES, i=PACK)
         planes = []
 
         def load_plane(n):
-            plane = sb([P, T], F32, "x%d" % n, tag="big%d" % n)
-            nc.sync.dma_start(out=plane[:], in_=x_rows[n // 4, n % 4])
+            plane = sbuf([P, T], F32, "plane%d" % n)
+            nc.sync.dma_start(out=plane[:], in_=x_rows[n // PACK, n % PACK])
             planes.append(plane)
 
+        def load_wval(a, first, width, name, tag=None):
+            raw = sbuf([P, PACK, width], F32, name, tag=tag)
+            rows = wval[a * PASS : (a + 1) * PASS, first : first + width]
+            nc.sync.dma_start(out=raw[:], in_=rows.rearrange("(p i) c -> p i c", i=PACK))
+            return raw
+
+        def round_wval(copy, dst, raw):
+            copy(out=dst.rearrange("p t m i -> p m i t"), in_=raw[:].rearrange("p i (m t) -> p m i t", t=PACK))
+
+        wval_bf = {}
+        wval_q = {}
+
+        def new_wval_bf(a, b):
+            wval_bf[a, b] = sbuf([P, PACK, P, PACK], BF16, "wval_bf%d%d" % (a, b))
+            return wval_bf[a, b]
+
+        def quantize_wval(a, b, tag=None):
+            woven = wval_bf[a, b][:].rearrange("p t m i -> p (t m i)")
+            wval_q[a, b] = quantize("wval_q%d%d" % (a, b), woven, PASS, tag=tag)
+
         load_plane(0)
-        nc.sync.dma_start(out=wgt_sb[:, QUARTER:], in_=wgt[:, QUARTER:])
-        for n in range(1, 7):
+        nc.sync.dma_start(out=weights[:, QUARTER:], in_=wgt[:, QUARTER:])
+        for n in range(1, PLANES - 1):
             load_plane(n)
-        wv00 = []
+        first_piece = new_wval_bf(0, 0)
+        first_piece_lo = load_wval(0, 0, PASS // 2, "first_piece_lo")
+        load_plane(PLANES - 1)
+        first_piece_hi = load_wval(0, PASS // 2, PASS // 2, "first_piece_hi")
+        gate_bias = sbuf([P, PASSES, PACK], F32, "gate_bias")
+        nc.sync.dma_start(out=gate_bias[:], in_=bgate.rearrange("(b p t) -> p b t", b=PASSES, t=PACK))
 
-        def load_wv00(part):
-            raw = sb([P, PACK, QUARTER], F32, "wv00_%d" % part)
-            cols = slice(part * QUARTER, (part + 1) * QUARTER)
-            nc.sync.dma_start(out=raw[:], in_=wval[:KP, cols].rearrange("(p j) c -> p j c", j=PACK))
-            wv00.append(raw)
-
-        wb00 = sb([P, PACK, P, PACK], BF16, "wv_bf00")
-        wv_bf[0, 0] = wb00[:].rearrange("p t m j -> p (t m j)")
-
-        def round_wv00(copy, part):
-            copy(
-                out=wb00[:, :, part * 64 : (part + 1) * 64, :].rearrange("p t m j -> p m j t"),
-                in_=wv00[part][:].rearrange("p j (m t) -> p m j t", t=PACK),
-            )
-
-        load_wv00(0)
-        load_plane(7)
-        load_wv00(1)
-        bg = sb([P, 2, PACK], F32, "bg")
-        nc.sync.dma_start(out=bg[:], in_=bgate.rearrange("(b p t) -> p b t", b=2, t=PACK))
-
-        gw = sb([P, 2 * 2 * H], U8, "gw")
+        groups = PASSES * PASSES
+        gate_words = sbuf([P, PASSES * 2 * H], U8, "gate_words")
         nc.vector.tensor_copy(
-            out=gw[:].bitcast(U16).rearrange("p (g t u v) -> p g u t v", g=4, t=4, v=8),
-            in_=gw_raw[:].bitcast(U16).rearrange("p (g u v t) -> p g u t v", g=4, t=4, v=8),
+            out=gate_words[:].bitcast(U16).rearrange("p (g t u v) -> p g u t v", g=groups, t=PACK, v=LINE // 2),
+            in_=gate_words_raw[:].bitcast(U16).rearrange("p (g u v t) -> p g u t v", g=groups, t=PACK, v=LINE // 2),
         )
-        gs = sb([P, 2 * H], U8, "gs")
+        gate_scales = sbuf([P, PASSES * H], U8, "gate_scales")
         nc.vector.tensor_copy(
-            out=gs[:].rearrange("p (g t u v) -> p g u t v", g=4, t=4, v=16),
-            in_=gs_raw[:].rearrange("p (g u v t) -> p g u t v", g=4, t=4, v=16),
+            out=gate_scales[:].rearrange("p (g t u v) -> p g u t v", g=groups, t=PACK, v=LINE),
+            in_=gate_scales_raw[:].rearrange("p (g u v t) -> p g u t v", g=groups, t=PACK, v=LINE),
         )
 
-        def gather(dst, n, lo, hi):
-            nc.vector.tensor_tensor(
-                dst[:, n % 4, lo:hi], planes[n][:].indirect(offsets[:, lo // 16 : hi // 16]), wgt_sb[:, lo:hi], MULT
-            )
+        def gather(picked, n, lo, hi):
+            window = planes[n][:].indirect(offsets[:, lo // LIST_ROWS : hi // LIST_ROWS])
+            nc.vector.tensor_tensor(picked[:, n % PACK, lo:hi], window, weights[:, lo:hi], MULT)
 
-        xq = {}
-        picked0 = sb([P, PACK, S], F32, "picked0")
+        xg_q = {}
+        picked0 = sbuf([P, PACK, S], F32, "picked0")
         gather(picked0, 0, 0, QUARTER)
         gather(picked0, 0, QUARTER, HALF)
         gather(picked0, 0, HALF, S)
-        for n in range(1, 4):
+        for n in range(1, PACK):
             gather(picked0, n, 0, S)
-        shared = sb([P, PACK * S], F32, "shared")
-        picked1 = shared[:].rearrange("p (t j) -> p t j", t=PACK)
-        xb0 = []
-        for hf in range(2):
-            xb = sb([P, HALF, PACK], BF16, "xb0_%d" % hf)
-            weave(nc.scalar.copy, xb[:], picked0[:, :, hf * HALF : (hf + 1) * HALF])
-            gather(picked1, 4 + hf, 0, S)
-            xb0.append(xb[:].rearrange("p j t -> p (j t)"))
-        gather(picked1, 6, 0, S)
-        xq[0, 0] = quantize("xq0_0", xb0[0], HALF, tag="big6")
-        round_wv00(nc.scalar.copy, 0)
-        gather(picked1, 7, 0, QUARTER)
-        gather(picked1, 7, QUARTER, HALF)
+        picked1_flat = sbuf([P, PACK * S], F32, "picked1")
+        picked1 = picked1_flat[:].rearrange("p (i j) -> p i j", i=PACK)
+        woven0 = []
+        for half in range(2):
+            woven = sbuf([P, HALF, PACK], BF16, "woven0_%d" % half)
+            weave(nc.scalar.copy, woven[:], picked0[:, :, half * HALF : (half + 1) * HALF])
+            gather(picked1, PACK + half, 0, S)
+            woven0.append(woven[:].rearrange("p j i -> p (j i)"))
+        gather(picked1, PLANES - 2, 0, S)
+        round_wval(nc.scalar.copy, first_piece[:, :, : P // 2, :], first_piece_lo)
+        xg_q[0, 0] = quantize("xg_q00", woven0[0], HALF, tag="first_piece_lo")
+        gather(picked1, PLANES - 1, 0, QUARTER)
+        gather(picked1, PLANES - 1, QUARTER, HALF)
 
-        def gate_pass(bank, a, b, t, hf):
-            col = (a * 2 + b) * HALF + t * P
-            codes, scales = xq[a, hf]
+        def gate_pass(bank, a, b, t, half):
+            col = (a * PASSES + b) * PASS + t * P
+            codes, scales = xg_q[a, half]
             nc.tensor.matmul_mx(
                 out=bank[:],
-                lhsT=gw[:, 2 * col : 2 * (col + P)].bitcast(FP4X4),
-                lhsT_scale=gs[:, col : col + P],
+                lhsT=gate_words[:, 2 * col : 2 * (col + P)].bitcast(FP4X4),
+                lhsT_scale=gate_scales[:, col : col + P],
                 rhs=codes[:].bitcast(FP8X4),
                 rhs_scale=scales[:],
                 start=(a == 0),
-                stop=(a == 1),
+                stop=(a == PASSES - 1),
             )
 
-        gate_banks = [next_bank([P, HALF]) for u in range(8)]
-        for u in range(8):
-            gate_pass(gate_banks[u], 0, u // 4, u % 4, 0)
+        row_tiles = [(b, t) for b in range(PASSES) for t in range(PACK)]
+        gate_banks = [next_bank([P, HALF]) for b, t in row_tiles]
+        for bank, (b, t) in zip(gate_banks, row_tiles):
+            gate_pass(bank, 0, b, t, 0)
 
-        codes = sb([P, HALF], U32, "xq1_0_codes")
-        scales = sb([P, HALF], U8, "xq1_0_scales")
-        xq[1, 0] = codes, scales
-        by_scalar = shared[:, PACK * S - HALF :].bitcast(BF16)
-        by_vector = sb([P, QUARTER * PACK], BF16, "by_vector")
-        weave(nc.scalar.copy, by_scalar.rearrange("p (j t) -> p j t", t=PACK), picked1[:, :, :QUARTER])
-        weave(nc.vector.tensor_copy, by_vector[:].rearrange("p (j t) -> p j t", t=PACK), picked1[:, :, QUARTER:HALF])
-        nc.vector.quantize_mx(out=codes[:, :QUARTER].bitcast(FP8X4), scales=scales[:, :QUARTER], in_=by_scalar)
-        nc.vector.quantize_mx(out=codes[:, QUARTER:].bitcast(FP8X4), scales=scales[:, QUARTER:], in_=by_vector[:])
-        round_wv00(nc.scalar.copy, 1)
-        gather(picked1, 7, HALF, S)
-        xq[0, 1] = quantize("xq0_1", xb0[1], HALF, tag="big7")
-        xb = sb([P, HALF, PACK], BF16, "xb1_1")
-        weave(nc.scalar.copy, xb[:, :QUARTER], picked1[:, :, HALF : HALF + QUARTER])
-        weave(nc.vector.tensor_copy, xb[:, QUARTER:], picked1[:, :, HALF + QUARTER :])
-        xq[1, 1] = quantize("xq1_1", xb[:].rearrange("p j t -> p (j t)"), HALF)
+        xg_q[1, 0] = sbuf([P, HALF], U32, "xg_q10_codes"), sbuf([P, HALF], U8, "xg_q10_scales")
+        quarters = [picked1_flat[:, PACK * S - HALF :].bitcast(BF16), sbuf([P, QUARTER * PACK], BF16, "quarter1")[:]]
+        for q, woven in enumerate(quarters):
+            tokens = slice(q * QUARTER, (q + 1) * QUARTER)
+            weave(nc.vector.tensor_copy, woven.rearrange("p (j i) -> p j i", i=PACK), picked1[:, :, tokens])
+        for q, woven in enumerate(quarters):
+            tokens = slice(q * QUARTER, (q + 1) * QUARTER)
+            codes, scales = xg_q[1, 0]
+            nc.vector.quantize_mx(out=codes[:, tokens].bitcast(FP8X4), scales=scales[:, tokens], in_=woven)
+        round_wval(nc.scalar.copy, first_piece[:, :, P // 2 :, :], first_piece_hi)
+        gather(picked1, PLANES - 1, HALF, S)
+        xg_q[0, 1] = quantize("xg_q01", woven0[1], HALF, tag="quarter1")
 
-        load_wval(1, 0)
-        load_wval(0, 1)
-        load_wval(1, 1)
-        round_wval(nc.vector.tensor_copy, 1, 0)
-        quantize_wval(0, 0, tag="xb0_1")
-        round_wval(nc.vector.tensor_copy, 0, 1)
+        woven = sbuf([P, HALF, PACK], BF16, "woven1_1")
+        weave(nc.scalar.copy, woven[:, :QUARTER], picked1[:, :, HALF : HALF + QUARTER])
+        weave(nc.vector.tensor_copy, woven[:, QUARTER:], picked1[:, :, HALF + QUARTER :])
+        quantize_wval(0, 0, tag="woven0_1")
+        xg_q[1, 1] = quantize("xg_q11", woven[:].rearrange("p j i -> p (j i)"), HALF)
+
+        wval_raw = {}
+        for slot, (a, b) in enumerate([(1, 0), (0, 1), (1, 1)]):
+            wval_raw[a, b] = load_wval(a, b * PASS, PASS, "wval_raw%d%d" % (a, b), tag="plane%d" % (slot + 1))
+        round_wval(nc.vector.tensor_copy, new_wval_bf(1, 0)[:], wval_raw[1, 0])
+        round_wval(nc.vector.tensor_copy, new_wval_bf(0, 1)[:], wval_raw[0, 1])
         quantize_wval(1, 0)
-        round_wval(nc.vector.tensor_copy, 1, 1)
+        round_wval(nc.vector.tensor_copy, new_wval_bf(1, 1)[:], wval_raw[1, 1])
         quantize_wval(0, 1)
-        quantize_wval(1, 1)
 
-        pw = sb([P, 2 * N], U32, "pw")
+        proj_words = sbuf([P, PASSES * N], U32, "proj_words")
         nc.sync.dma_start(
-            out=pw[:].bitcast(I32).rearrange("p (a c) -> p a c", a=2),
-            in_=wproj_words.rearrange("a p c i -> p a (c i)").bitcast(I32),
+            out=proj_words[:].bitcast(I32).rearrange("p (b c) -> p b c", b=PASSES),
+            in_=wproj_words.rearrange("b p c t -> p b (c t)").bitcast(I32),
         )
-        load_scale_rows(ps_plane, wproj_scales)
-        bp = sb([P, N // P], F32, "bp")
-        with nc.allow_non_contiguous_dma(reason="one bias value a partition"):
-            nc.sync.dma_start(out=bp[:], in_=bproj.rearrange("(i p) -> p i", p=P))
+        load_scale_rows(proj_scales, wproj_scales)
+        proj_bias = sbuf([P, OUT_TILES], F32, "proj_bias")
+        with nc.allow_non_contiguous_dma(reason="one bias value a partition for each tile of 128 output rows"):
+            nc.sync.dma_start(out=proj_bias[:], in_=bproj.rearrange("(o p) -> p o", p=P))
 
-        sig = {}
+        gates = {}
+        gate_tags = {(0, 0): "plane4", (1, 0): "plane5", (0, 1): "plane0", (1, 1): None}
 
-        def sigmoid(bank, b, t, hf):
+        def sigmoid(bank, b, t, half):
             if t == 0:
-                sig[b, hf] = sb([P, PACK, HALF], F32, "sig%d%d" % (b, hf), tag=("big4", "big5", "big0", None)[2 * hf + b])
-            nc.scalar.activation(sig[b, hf][:, t, :], bank[:], SIGMOID, bias=bg[:, b, t : t + 1])
+                gates[b, half] = sbuf([P, PACK, HALF], F32, "gates%d%d" % (b, half), tag=gate_tags[b, half])
+            nc.scalar.activation(gates[b, half][:, t, :], bank[:], SIGMOID, bias=gate_bias[:, b, t : t + 1])
 
-        for u in range(8):
-            gate_pass(gate_banks[u], 1, u // 4, u % 4, 0)
-            sigmoid(gate_banks[u], u // 4, u % 4, 0)
+        for bank, (b, t) in zip(gate_banks, row_tiles):
+            gate_pass(bank, 1, b, t, 0)
+            sigmoid(bank, b, t, 0)
 
-        gate_banks = [next_bank([P, HALF]) for u in range(8)]
-        for u in range(8):
-            gate_pass(gate_banks[u], 0, u // 4, u % 4, 1)
-        for u in range(8):
-            gate_pass(gate_banks[u], 1, u // 4, u % 4, 1)
-            sigmoid(gate_banks[u], u // 4, u % 4, 1)
+        gate_banks = [next_bank([P, HALF]) for b, t in row_tiles]
+        for bank, (b, t) in zip(gate_banks, row_tiles):
+            gate_pass(bank, 0, b, t, 1)
+        for bank, (b, t) in zip(gate_banks, row_tiles):
+            gate_pass(bank, 1, b, t, 1)
+            sigmoid(bank, b, t, 1)
 
-        def hidden(b, lo, width):
-            hf, base = divmod(lo, HALF)
-            hb = sb([P, width, PACK], BF16, "hb%d_%d" % (b, lo))
-            for c in range(0, width, CHUNK):
+        h_q = {}
+
+        def hidden(b, lo, width, waiting):
+            half, base = divmod(lo, HALF)
+            h_bf = sbuf([P, width, PACK], BF16, "h_bf%d_%d" % (b, lo))
+            for c0 in range(0, width, CHUNK):
                 bank = next_bank([P, PACK, CHUNK])
-                cols = slice(base + c, base + c + CHUNK)
+                tokens = slice(base + c0, base + c0 + CHUNK)
                 for t in range(PACK):
-                    for a in range(2):
-                        w_codes, w_scales = wq[a, b]
-                        codes, scales = xq[a, hf]
+                    for a in range(PASSES):
+                        w_codes, w_scales = wval_q[a, b]
+                        codes, scales = xg_q[a, half]
                         nc.tensor.matmul_mx(
                             out=bank[:, t, :],
                             lhsT=w_codes[:, t * P : (t + 1) * P].bitcast(FP8X4),
                             lhsT_scale=w_scales[:, t * P : (t + 1) * P],
-                            rhs=codes[:, cols].bitcast(FP8X4),
-                            rhs_scale=scales[:, cols],
+                            rhs=codes[:, tokens].bitcast(FP8X4),
+                            rhs_scale=scales[:, tokens],
                             start=(a == 0),
-                            stop=(a == 1),
+                            stop=(a == PASSES - 1),
                         )
                 nc.vector.tensor_tensor(
-                    hb[:, c : c + CHUNK, :].rearrange("p (c i) t -> p c t i", i=2),
-                    bank[:].rearrange("p t (c i) -> p c t i", i=2),
-                    sig[b, hf][:, :, cols].rearrange("p t (c i) -> p c t i", i=2),
+                    h_bf[:, c0 : c0 + CHUNK, :].rearrange("p (c e) t -> p c t e", e=2),
+                    bank[:].rearrange("p t (c e) -> p c t e", e=2),
+                    gates[b, half][:, :, tokens].rearrange("p t (c e) -> p c t e", e=2),
                     MULT,
                 )
-            return quantize("hq%d_%d" % (b, lo), hb[:].rearrange("p j t -> p (j t)"), width)
+                if c0 == 0:
+                    waiting()
 
-        out_rows = out.rearrange("(i p) j -> p i j", p=P)
+            def quantize_h():
+                h_q[b, lo] = quantize("h_q%d_%d" % (b, lo), h_bf[:].rearrange("p j t -> p (j t)"), width)
 
-        def project(hq, lo, width, last):
+            return quantize_h
+
+        out_rows = out.rearrange("(o p) j -> p o j", p=P)
+
+        def project(lo, width, share_with_vector):
             per_bank = min(HALF // width, 2)
-            for i0 in range(0, N // P, per_bank):
-                bank = next_bank([P, per_bank, width])
-                res = sb([P, per_bank, width], F32, "res%d_%d" % (lo, i0))
-                for i in range(i0, i0 + per_bank):
-                    for b in range(2):
-                        codes, scales, c0 = hq[b]
-                        col = b * N + i * P
-                        nc.tensor.matmul_mx(
-                            out=bank[:, i - i0, :],
-                            lhsT=pw[:, col : col + P].bitcast(FP8X4),
-                            lhsT_scale=ps_plane[:, col : col + P],
-                            rhs=codes[:, c0 : c0 + width].bitcast(FP8X4),
-                            rhs_scale=scales[:, c0 : c0 + width],
-                            start=(b == 0),
-                            stop=(b == 1),
-                        )
-                for i in range(i0, i0 + per_bank):
-                    if last and i0 > 0:
-                        nc.vector.tensor_scalar(res[:, i - i0, :], bank[:, i - i0, :], bp[:, i : i + 1], None, ADD)
+            firsts = range(0, OUT_TILES, per_bank)
+            banks = [next_bank([P, per_bank, width]) for first in firsts]
+            for b in range(PASSES):
+                h_lo = max(start for block, start in h_q if block == b and start <= lo)
+                codes, scales = h_q[b, h_lo]
+                tokens = slice(lo - h_lo, lo - h_lo + width)
+                for o in range(OUT_TILES):
+                    col = b * N + o * P
+                    nc.tensor.matmul_mx(
+                        out=banks[o // per_bank][:, o % per_bank, :],
+                        lhsT=proj_words[:, col : col + P].bitcast(FP8X4),
+                        lhsT_scale=proj_scales[:, col : col + P],
+                        rhs=codes[:, tokens].bitcast(FP8X4),
+                        rhs_scale=scales[:, tokens],
+                        start=(b == 0 and o % per_bank == 0),
+                        stop=(b == PASSES - 1 and o % per_bank == per_bank - 1),
+                    )
+            for bank, first in zip(banks, firsts):
+                result = sbuf([P, per_bank, width], F32, "result%d_%d" % (lo, first))
+                for slot in range(per_bank):
+                    bias = proj_bias[:, first + slot : first + slot + 1]
+                    if share_with_vector and first > 0:
+                        nc.vector.tensor_scalar(result[:, slot, :], bank[:, slot, :], bias, None, ADD)
                     else:
-                        nc.scalar.activation(res[:, i - i0, :], bank[:, i - i0, :], IDENTITY, bias=bp[:, i : i + 1])
-                nc.sync.dma_start(out=out_rows[:, i0 : i0 + per_bank, lo : lo + width], in_=res[:])
+                        nc.scalar.activation(result[:, slot, :], bank[:, slot, :], IDENTITY, bias=bias)
+                nc.sync.dma_start(out=out_rows[:, first : first + per_bank, lo : lo + width], in_=result[:])
 
-        h00 = hidden(0, 0, HALF)
-        h10 = hidden(1, 0, HALF)
-        h01 = hidden(0, HALF, HALF)
-        h12 = hidden(1, HALF, QUARTER)
-        project([h00 + (0,), h10 + (0,)], 0, HALF, False)
-        h13 = hidden(1, HALF + QUARTER, CHUNK)
-        h14 = hidden(1, HALF + QUARTER + CHUNK, CHUNK)
-        project([h01 + (0,), h12 + (0,)], HALF, QUARTER, False)
-        project([h01 + (QUARTER,), h13 + (0,)], HALF + QUARTER, CHUNK, False)
-        project([h01 + (QUARTER + CHUNK,), h14 + (0,)], HALF + QUARTER + CHUNK, CHUNK, True)
+        last_quarter = HALF + QUARTER
+        waiting = hidden(0, 0, HALF, lambda: quantize_wval(1, 1))
+        waiting = hidden(1, 0, HALF, waiting)
+        waiting = hidden(0, HALF, QUARTER, waiting)
+        waiting = hidden(1, HALF, QUARTER, waiting)
+        project(0, HALF, False)
+        waiting = hidden(0, last_quarter, QUARTER, waiting)
+        waiting = hidden(1, last_quarter, CHUNK, waiting)
+        project(HALF, QUARTER, False)
+        waiting = hidden(1, last_quarter + CHUNK, CHUNK, waiting)
+        waiting()
+        project(last_quarter, CHUNK, False)
+        project(last_quarter + CHUNK, CHUNK, True)

from contextlib import ExitStack

import concourse.mybir as mybir

K, T, S, H, N = 1024, 2048, 1024, 1024, 512
FLOPS = 2 * K * H * S * 2 + 2 * H * N * S

F32 = mybir.dt.float32
BF16 = mybir.dt.bfloat16
I32 = mybir.dt.int32
U32 = mybir.dt.uint32
U16 = mybir.dt.uint16
U8 = mybir.dt.uint8
FP8X4 = mybir.dt.float8_e4m3fn_x4
FP4X4 = mybir.dt.float4_e2m1fn_x4
MULT = mybir.AluOpType.mult
ADD = mybir.AluOpType.add
SIGMOID = mybir.ActivationFunctionType.Sigmoid
IDENTITY = mybir.ActivationFunctionType.Identity

P = 128
PACK = 4
PASS = P * PACK
PASSES = 2
PLANES = PASSES * PACK
HALF = S // 2
QUARTER = S // 4
CHUNK = HALF // PACK
LIST_ROWS = 16
BANKS = 8
OUT_TILES = N // P
LINE = 16


def tile_list_head_picked_glu_kernel(
    tc, xT, wgt, offs, wgate_words, wgate_scales, bgate, wval, wproj_words, wproj_scales, bproj, out
):
    nc = tc.nc
    with ExitStack() as ctx:
        keep = ctx.enter_context(tc.tile_pool(name="keep", bufs=1))
        psum = ctx.enter_context(tc.psum_pool(name="psum", bufs=1))
        banks_taken = []

        def next_bank(shape):
            index = len(banks_taken) % BANKS
            banks_taken.append(index)
            return psum.tile(shape, F32, name="bank%d" % index)

        def sbuf(shape, dtype, name, tag=None):
            return keep.tile(shape, dtype, name=name, tag=tag or name, align_bytes=64)

        def load_scale_rows(scale_tile, scale_rows):
            src = scale_rows.bitcast(I32)
            dst = scale_tile[:].bitcast(I32).rearrange("p (a c) -> p a c", a=PASSES)
            for quad in range(4):
                nc.sync.dma_start(
                    out=dst[32 * quad : 32 * quad + 4],
                    in_=src[:, 4 * quad : 4 * quad + 4, :].rearrange("a s c -> s a c"),
                )

        def weave(copy, dst, src):
            copy(out=dst.rearrange("p (c e) i -> p c i e", e=4), in_=src.rearrange("p i (c e) -> p c i e", e=4))

        def quantize(name, woven, width, tag=None):
            codes = sbuf([P, width], U32, name + "_codes", tag=tag)
            scales = sbuf([P, width], U8, name + "_scales")
            nc.vector.quantize_mx(out=codes[:].bitcast(FP8X4), scales=scales[:], in_=woven)
            return codes, scales

        gate_scales_raw = sbuf([P, PASSES * H], U8, "gate_scales_raw")
        nc.vector.memset(gate_scales_raw[:].bitcast(I32), 0)
        proj_scales = sbuf([P, PASSES * N], U8, "proj_scales")
        nc.gpsimd.memset(proj_scales[:].bitcast(I32), 0)

        offsets = keep.tile([P, S // LIST_ROWS], U16, name="offsets")
        nc.sync.dma_start(offsets[:], offs)
        gate_words_raw = sbuf([P, PASSES * 2 * H], U8, "gate_words_raw")
        nc.sync.dma_start(
            out=gate_words_raw[:].bitcast(I32).rearrange("p (a c) -> p a c", a=PASSES),
            in_=wgate_words.bitcast(I32).rearrange("a p c -> p a c"),
        )
        load_scale_rows(gate_scales_raw, wgate_scales)
        weights = sbuf([P, S], F32, "weights")
        nc.sync.dma_start(out=weights[:, :QUARTER], in_=wgt[:, :QUARTER])

        x_rows = xT.rearrange("(a p i) t -> a i p t", a=PASSES, i=PACK)
        planes = []

        def load_plane(n):
            plane = sbuf([P, T], F32, "plane%d" % n)
            nc.sync.dma_start(out=plane[:], in_=x_rows[n // PACK, n % PACK])
            planes.append(plane)

        def load_wval(a, first, width, name, tag=None):
            raw = sbuf([P, PACK, width], F32, name, tag=tag)
            rows = wval[a * PASS : (a + 1) * PASS, first : first + width]
            nc.sync.dma_start(out=raw[:], in_=rows.rearrange("(p i) c -> p i c", i=PACK))
            return raw

        def round_wval(copy, dst, raw):
            copy(out=dst.rearrange("p t m i -> p m i t"), in_=raw[:].rearrange("p i (m t) -> p m i t", t=PACK))

        wval_bf = {}
        wval_q = {}

        def new_wval_bf(a, b):
            wval_bf[a, b] = sbuf([P, PACK, P, PACK], BF16, "wval_bf%d%d" % (a, b))
            return wval_bf[a, b]

        def quantize_wval(a, b, tag=None):
            woven = wval_bf[a, b][:].rearrange("p t m i -> p (t m i)")
            wval_q[a, b] = quantize("wval_q%d%d" % (a, b), woven, PASS, tag=tag)

        load_plane(0)
        nc.sync.dma_start(out=weights[:, QUARTER:], in_=wgt[:, QUARTER:])
        for n in range(1, PLANES - 1):
            load_plane(n)
        first_piece = new_wval_bf(0, 0)
        first_piece_lo = load_wval(0, 0, PASS // 2, "first_piece_lo")
        load_plane(PLANES - 1)
        first_piece_hi = load_wval(0, PASS // 2, PASS // 2, "first_piece_hi")
        gate_bias = sbuf([P, PASSES, PACK], F32, "gate_bias")
        nc.sync.dma_start(out=gate_bias[:], in_=bgate.rearrange("(b p t) -> p b t", b=PASSES, t=PACK))

        groups = PASSES * PASSES
        gate_words = sbuf([P, PASSES * 2 * H], U8, "gate_words")
        nc.vector.tensor_copy(
            out=gate_words[:].bitcast(U16).rearrange("p (g t u v) -> p g u t v", g=groups, t=PACK, v=LINE // 2),
            in_=gate_words_raw[:].bitcast(U16).rearrange("p (g u v t) -> p g u t v", g=groups, t=PACK, v=LINE // 2),
        )
        gate_scales = sbuf([P, PASSES * H], U8, "gate_scales")
        nc.vector.tensor_copy(
            out=gate_scales[:].rearrange("p (g t u v) -> p g u t v", g=groups, t=PACK, v=LINE),
            in_=gate_scales_raw[:].rearrange("p (g u v t) -> p g u t v", g=groups, t=PACK, v=LINE),
        )

        def gather(picked, n, lo, hi):
            window = planes[n][:].indirect(offsets[:, lo // LIST_ROWS : hi // LIST_ROWS])
            nc.vector.tensor_tensor(picked[:, n % PACK, lo:hi], window, weights[:, lo:hi], MULT)

        xg_q = {}
        picked0 = sbuf([P, PACK, S], F32, "picked0")
        gather(picked0, 0, 0, QUARTER)
        gather(picked0, 0, QUARTER, HALF)
        gather(picked0, 0, HALF, S)
        for n in range(1, PACK):
            gather(picked0, n, 0, S)
        picked1_flat = sbuf([P, PACK * S], F32, "picked1")
        picked1 = picked1_flat[:].rearrange("p (i j) -> p i j", i=PACK)
        woven0 = []
        for half in range(2):
            woven = sbuf([P, HALF, PACK], BF16, "woven0_%d" % half)
            weave(nc.scalar.copy, woven[:], picked0[:, :, half * HALF : (half + 1) * HALF])
            gather(picked1, PACK + half, 0, S)
            woven0.append(woven[:].rearrange("p j i -> p (j i)"))
        gather(picked1, PLANES - 2, 0, S)
        round_wval(nc.scalar.copy, first_piece[:, :, : P // 2, :], first_piece_lo)
        xg_q[0, 0] = quantize("xg_q00", woven0[0], HALF, tag="first_piece_lo")
        gather(picked1, PLANES - 1, 0, QUARTER)
        gather(picked1, PLANES - 1, QUARTER, HALF)

        def gate_pass(bank, a, b, t, half):
            col = (a * PASSES + b) * PASS + t * P
            codes, scales = xg_q[a, half]
            nc.tensor.matmul_mx(
                out=bank[:],
                lhsT=gate_words[:, 2 * col : 2 * (col + P)].bitcast(FP4X4),
                lhsT_scale=gate_scales[:, col : col + P],
                rhs=codes[:].bitcast(FP8X4),
                rhs_scale=scales[:],
                start=(a == 0),
                stop=(a == PASSES - 1),
            )

        row_tiles = [(b, t) for b in range(PASSES) for t in range(PACK)]
        gate_banks = [next_bank([P, HALF]) for b, t in row_tiles]
        for bank, (b, t) in zip(gate_banks, row_tiles):
            gate_pass(bank, 0, b, t, 0)

        xg_q[1, 0] = sbuf([P, HALF], U32, "xg_q10_codes"), sbuf([P, HALF], U8, "xg_q10_scales")
        quarters = [picked1_flat[:, PACK * S - HALF :].bitcast(BF16), sbuf([P, QUARTER * PACK], BF16, "quarter1")[:]]
        for q, woven in enumerate(quarters):
            tokens = slice(q * QUARTER, (q + 1) * QUARTER)
            weave(nc.vector.tensor_copy, woven.rearrange("p (j i) -> p j i", i=PACK), picked1[:, :, tokens])
        for q, woven in enumerate(quarters):
            tokens = slice(q * QUARTER, (q + 1) * QUARTER)
            codes, scales = xg_q[1, 0]
            nc.vector.quantize_mx(out=codes[:, tokens].bitcast(FP8X4), scales=scales[:, tokens], in_=woven)
        round_wval(nc.scalar.copy, first_piece[:, :, P // 2 :, :], first_piece_hi)
        gather(picked1, PLANES - 1, HALF, S)
        xg_q[0, 1] = quantize("xg_q01", woven0[1], HALF, tag="quarter1")

        woven = sbuf([P, HALF, PACK], BF16, "woven1_1")
        weave(nc.scalar.copy, woven[:, :QUARTER], picked1[:, :, HALF : HALF + QUARTER])
        weave(nc.vector.tensor_copy, woven[:, QUARTER:], picked1[:, :, HALF + QUARTER :])
        quantize_wval(0, 0, tag="woven0_1")
        xg_q[1, 1] = quantize("xg_q11", woven[:].rearrange("p j i -> p (j i)"), HALF)

        wval_raw = {}
        for slot, (a, b) in enumerate([(1, 0), (0, 1), (1, 1)]):
            wval_raw[a, b] = load_wval(a, b * PASS, PASS, "wval_raw%d%d" % (a, b), tag="plane%d" % (slot + 1))
        round_wval(nc.vector.tensor_copy, new_wval_bf(1, 0)[:], wval_raw[1, 0])
        round_wval(nc.vector.tensor_copy, new_wval_bf(0, 1)[:], wval_raw[0, 1])
        quantize_wval(1, 0)
        round_wval(nc.vector.tensor_copy, new_wval_bf(1, 1)[:], wval_raw[1, 1])
        quantize_wval(0, 1)

        proj_words = sbuf([P, PASSES * N], U32, "proj_words")
        nc.sync.dma_start(
            out=proj_words[:].bitcast(I32).rearrange("p (b c) -> p b c", b=PASSES),
            in_=wproj_words.rearrange("b p c t -> p b (c t)").bitcast(I32),
        )
        load_scale_rows(proj_scales, wproj_scales)
        proj_bias = sbuf([P, OUT_TILES], F32, "proj_bias")
        with nc.allow_non_contiguous_dma(reason="one bias value a partition for each tile of 128 output rows"):
            nc.sync.dma_start(out=proj_bias[:], in_=bproj.rearrange("(o p) -> p o", p=P))

        gates = {}
        gate_tags = {(0, 0): "plane4", (1, 0): "plane5", (0, 1): "plane0", (1, 1): None}

        def sigmoid(bank, b, t, half):
            if t == 0:
                gates[b, half] = sbuf([P, PACK, HALF], F32, "gates%d%d" % (b, half), tag=gate_tags[b, half])
            nc.scalar.activation(gates[b, half][:, t, :], bank[:], SIGMOID, bias=gate_bias[:, b, t : t + 1])

        for bank, (b, t) in zip(gate_banks, row_tiles):
            gate_pass(bank, 1, b, t, 0)
            sigmoid(bank, b, t, 0)

        gate_banks = [next_bank([P, HALF]) for b, t in row_tiles]
        for bank, (b, t) in zip(gate_banks, row_tiles):
            gate_pass(bank, 0, b, t, 1)
        for bank, (b, t) in zip(gate_banks, row_tiles):
            gate_pass(bank, 1, b, t, 1)
            sigmoid(bank, b, t, 1)

        h_q = {}

        def hidden(b, lo, width, waiting):
            half, base = divmod(lo, HALF)
            h_bf = sbuf([P, width, PACK], BF16, "h_bf%d_%d" % (b, lo))
            for c0 in range(0, width, CHUNK):
                bank = next_bank([P, PACK, CHUNK])
                tokens = slice(base + c0, base + c0 + CHUNK)
                for t in range(PACK):
                    for a in range(PASSES):
                        w_codes, w_scales = wval_q[a, b]
                        codes, scales = xg_q[a, half]
                        nc.tensor.matmul_mx(
                            out=bank[:, t, :],
                            lhsT=w_codes[:, t * P : (t + 1) * P].bitcast(FP8X4),
                            lhsT_scale=w_scales[:, t * P : (t + 1) * P],
                            rhs=codes[:, tokens].bitcast(FP8X4),
                            rhs_scale=scales[:, tokens],
                            start=(a == 0),
                            stop=(a == PASSES - 1),
                        )
                nc.vector.tensor_tensor(
                    h_bf[:, c0 : c0 + CHUNK, :].rearrange("p (c e) t -> p c t e", e=2),
                    bank[:].rearrange("p t (c e) -> p c t e", e=2),
                    gates[b, half][:, :, tokens].rearrange("p t (c e) -> p c t e", e=2),
                    MULT,
                )
                if c0 == 0:
                    waiting()

            def quantize_h():
                h_q[b, lo] = quantize("h_q%d_%d" % (b, lo), h_bf[:].rearrange("p j t -> p (j t)"), width)

            return quantize_h

        out_rows = out.rearrange("(o p) j -> p o j", p=P)

        def project(lo, width, share_with_vector):
            per_bank = min(HALF // width, 2)
            firsts = range(0, OUT_TILES, per_bank)
            banks = [next_bank([P, per_bank, width]) for first in firsts]
            for b in range(PASSES):
                h_lo = max(start for block, start in h_q if block == b and start <= lo)
                codes, scales = h_q[b, h_lo]
                tokens = slice(lo - h_lo, lo - h_lo + width)
                for o in range(OUT_TILES):
                    col = b * N + o * P
                    nc.tensor.matmul_mx(
                        out=banks[o // per_bank][:, o % per_bank, :],
                        lhsT=proj_words[:, col : col + P].bitcast(FP8X4),
                        lhsT_scale=proj_scales[:, col : col + P],
                        rhs=codes[:, tokens].bitcast(FP8X4),
                        rhs_scale=scales[:, tokens],
                        start=(b == 0 and o % per_bank == 0),
                        stop=(b == PASSES - 1 and o % per_bank == per_bank - 1),
                    )
            for bank, first in zip(banks, firsts):
                result = sbuf([P, per_bank, width], F32, "result%d_%d" % (lo, first))
                for slot in range(per_bank):
                    bias = proj_bias[:, first + slot : first + slot + 1]
                    if share_with_vector and first > 0:
                        nc.vector.tensor_scalar(result[:, slot, :], bank[:, slot, :], bias, None, ADD)
                    else:
                        nc.scalar.activation(result[:, slot, :], bank[:, slot, :], IDENTITY, bias=bias)
                nc.sync.dma_start(out=out_rows[:, first : first + per_bank, lo : lo + width], in_=result[:])

        last_quarter = HALF + QUARTER
        waiting = hidden(0, 0, HALF, lambda: quantize_wval(1, 1))
        waiting = hidden(1, 0, HALF, waiting)
        waiting = hidden(0, HALF, QUARTER, waiting)
        waiting = hidden(1, HALF, QUARTER, waiting)
        project(0, HALF, False)
        waiting = hidden(0, last_quarter, QUARTER, waiting)
        waiting = hidden(1, last_quarter, CHUNK, waiting)
        project(HALF, QUARTER, False)
        waiting = hidden(1, last_quarter + CHUNK, CHUNK, waiting)
        waiting()
        project(last_quarter, CHUNK, False)
        project(last_quarter + CHUNK, CHUNK, True)
